import numpy as np
import ml_dtypes


def mxq(x, axis, fmt="e4m3"):
    dtype, down = {"e4m3": (ml_dtypes.float8_e4m3fn, 7), "e5m2": (ml_dtypes.float8_e5m2, 14)}[fmt]
    v = np.moveaxis(np.asarray(x, np.float32).astype(ml_dtypes.bfloat16).astype(np.float64), axis, -1)
    blocks = v.reshape(v.shape[:-1] + (-1, 32))
    amax = np.abs(blocks).max(-1, keepdims=True)
    byte = np.maximum(np.where(amax > 0, np.frexp(amax)[1] - 1 + 127, 0) - down, 1)
    scale = np.exp2(byte - 127.0)
    codes = (blocks / scale).astype(np.float32).astype(dtype).astype(np.float64)
    return np.moveaxis((codes * scale).reshape(v.shape), -1, axis)


WIDE = False


def mx_kscale(k):
    if not WIDE:
        return np.ones(k)
    levels = np.array([10, -10, 5, -5, 0])
    if k % 512:
        return np.exp2(np.random.permutation(np.resize(levels, k // 32))).repeat(32)
    a = np.empty((k // 512, 16))
    for p in range(k // 512):
        a[p, :8] = np.random.permutation(np.resize(levels, 8))
        for g in range(8):
            far = levels[np.abs(levels - a[p, g]) >= 10]
            a[p, g + 8] = far[np.random.randint(len(far))]
    return np.exp2(a.ravel()).repeat(32)


BF16 = ml_dtypes.bfloat16


def bf(x):
    return np.asarray(x, np.float32).astype(BF16)


def f64(x):
    return np.asarray(x).astype(np.float64)


E2M1 = np.array([0.0, 0.5, 1.0, 1.5, 2.0, 3.0, 4.0, 6.0, -0.0, -0.5, -1.0, -1.5, -2.0, -3.0, -4.0, -6.0])


def pack_weight(w, fmt):
    k, n = w.shape
    w = f64(bf(w)).reshape(k // 32, 32, n)
    amax = np.abs(w).max(1)
    if fmt == "e4m3":
        byte = np.frexp(amax)[1] - 1 + 127 - 7
    else:
        mant, ex = np.frexp(amax / 6.0)
        byte = np.where(mant > 0.5, ex, ex - 1) + 127
    byte = np.clip(np.where(amax > 0, byte, 1), 1, 254)
    scaled = (w * np.exp2(127.0 - byte)[:, None, :]).reshape(k, n).astype(np.float32)
    by_word = np.ascontiguousarray(scaled.reshape(k // 512, 128, 4, n).transpose(0, 1, 3, 2))
    if fmt == "e4m3":
        words = by_word.astype(ml_dtypes.float8_e4m3fn).view(np.uint8)
    else:
        c = by_word.astype(ml_dtypes.float4_e2m1fn).view(np.uint8) & 0xF
        words = c[..., 0::2] | (c[..., 1::2] << 4)
    return np.ascontiguousarray(words), np.ascontiguousarray(byte.astype(np.uint8).reshape(k // 512, 16, n))


def unpack_weight(words, scales, fmt):
    g, p, n, _ = words.shape
    if fmt == "e4m3":
        vals = np.ascontiguousarray(words).view(ml_dtypes.float8_e4m3fn).astype(np.float64)
    else:
        nib = np.empty((g, p, n, 4), np.uint8)
        nib[..., 0::2] = words & 0xF
        nib[..., 1::2] = words >> 4
        vals = E2M1[nib]
    vals = vals * np.repeat(np.exp2(scales.astype(np.float64) - 127.0), 8, axis=1)[..., None]
    return vals.transpose(0, 1, 3, 2).reshape(g * 512, n)
def pack4(w):
    words, scales = pack_weight(w, "e2m1")
    return words.reshape(words.shape[0], 128, -1), scales


def unpack4(words, scales):
    return unpack_weight(words.reshape(words.shape[0], 128, -1, 2), scales, "e2m1")


E4M3FN = np.array([(-1.0 if i & 128 else 1.0) * ((1.0 + (i & 7) / 8.0) * 2.0 ** (((i >> 3) & 15) - 7) if i & 120 else (i & 7) * 2.0 ** -9) for i in range(256)])


def e4m3fn_bytes(y):
    return np.clip(np.asarray(y, np.float64), -448.0, 448.0).astype(np.float32).astype(ml_dtypes.float8_e4m3fn).view(np.uint8)


def e4m3fn_values(b):
    return E4M3FN[b]


T, A, L, B = 1024, 1024, 2048, 128


def setup_inputs():
    s, t = mx_kscale(A), mx_kscale(L)
    C = np.random.standard_normal((T, A)) * s
    C_scale = (np.abs(C).reshape(T, A // B, B).max(axis=2) / 448).astype(np.float32)
    C_bytes = e4m3fn_bytes(C / np.repeat(f64(C_scale), B, axis=1))
    G_words, G_scales = pack4(np.random.standard_normal((A, L)) / np.sqrt(A) / s[:, None] * t)
    R = np.random.standard_normal((A, L)) / np.sqrt(L) / t
    R_scale = (np.abs(R).reshape(A // B, B, L // B, B).max(axis=(1, 3)) / 448).astype(np.float32)
    R_bytes = e4m3fn_bytes(R / np.repeat(np.repeat(f64(R_scale), B, axis=0), B, axis=1))
    return {"C_bytes": C_bytes, "C_scale": C_scale,
            "G_words": G_words, "G_scales": G_scales,
            "slopes": bf(np.random.standard_normal((T, L)) * t),
            "R_bytes": R_bytes, "R_scale": R_scale,
            "gain": bf(np.random.uniform(0.4, 0.8, A)),
            "leak": bf(np.random.uniform(0.6, 0.95, A)),
            "prev": bf(np.random.standard_normal((T, A)))}


def reference(C_bytes, C_scale, G_words, G_scales, slopes, R_bytes, R_scale, gain, leak, prev):
    C = e4m3fn_values(C_bytes) * np.repeat(f64(C_scale), B, axis=1)
    R = e4m3fn_values(R_bytes) * np.repeat(np.repeat(f64(R_scale), B, axis=0), B, axis=1)
    mirror = mxq(C, 1, "e4m3") @ unpack4(G_words, G_scales)
    full = f64(slopes) + mirror
    e = mxq(full, 1, "e4m3") @ mxq(R, 1, "e4m3").T
    return f64(leak) * f64(prev) + f64(gain) * e

@@ -1,0 +1,279 @@
+from contextlib import ExitStack
+
+import concourse.mybir as mybir
+from concourse.masks import make_identity
+
+T, A, L = 1024, 1024, 2048
+P = 128
+FLOPS = 2 * T * A * L * 2
+
+F32 = mybir.dt.float32
+BF16 = mybir.dt.bfloat16
+I32 = mybir.dt.int32
+U32 = mybir.dt.uint32
+U8 = mybir.dt.uint8
+FP8 = mybir.dt.float8_e4m3fn
+FP8X4 = mybir.dt.float8_e4m3fn_x4
+FP4X4 = mybir.dt.float4_e2m1fn_x4
+MULT = mybir.AluOpType.mult
+ADD = mybir.AluOpType.add
+COPY = mybir.ActivationFunctionType.Copy
+
+NT = T // P
+NR = A // P
+GA = A // 512
+GL = L // 512
+NL = L // 512
+NA = A // 512
+
+
+def tile_leaky_slope_reconstructor_d6_kernel(
+    tc, C_bytes, C_scale, G_words, G_scales, slopes, R_bytes, R_scale, gain, leak, prev, out
+):
+    nc = tc.nc
+    with ExitStack() as ctx:
+        keep = ctx.enter_context(tc.tile_pool(name="keep", bufs=1))
+        work = ctx.enter_context(tc.tile_pool(name="work", bufs=3))
+        psum = ctx.enter_context(tc.psum_pool(name="psum", bufs=1))
+
+        c_raw = keep.tile([P, NT, A], U8, align_bytes=64)
+        c_sc = keep.tile([P, NT, A // P], F32, align_bytes=64)
+        g_words = keep.tile([P, GA, 2 * L], U8, align_bytes=64)
+        g_sc = keep.tile([P, GA, L], U8, align_bytes=64)
+        r_raw = keep.tile([P, NR, L], U8, align_bytes=64)
+        r_sc = keep.tile([P, NR * (L // P)], F32, align_bytes=64)
+        s_sb = keep.tile([P, NT, L], BF16, align_bytes=64)
+        prev_sb = keep.tile([P, NT, A], BF16, align_bytes=64)
+        gain_sb = keep.tile([P, A], BF16, align_bytes=64)
+        leak_sb = keep.tile([P, A], BF16, align_bytes=64)
+        ident = keep.tile([P, P], F32, align_bytes=64)
+        c_codes = keep.tile([P, NT, GA * P], U32, align_bytes=64)
+        c_planes = keep.tile([P, NT, GA * P], U8, align_bytes=64)
+        r_codes = keep.tile([P, GL, A], U32, align_bytes=64)
+        r_planes = keep.tile([P, GL, A], U8, align_bytes=64)
+        f_codes = keep.tile([P, NT, GL * P], U32, align_bytes=64)
+        f_planes = keep.tile([P, NT, GL * P], U8, align_bytes=64)
+
+        c_v = C_bytes.rearrange("(p i) k -> p i k", i=NT)
+        s_v = slopes.rearrange("(p i) l -> p i l", i=NT)
+        p_v = prev.rearrange("(p i) a -> p i a", i=NT)
+        o_v = out.rearrange("(p i) a -> p i a", i=NT)
+        r_v = R_bytes.rearrange("(i p) l -> p i l", p=P)
+
+        make_identity(nc, ident[:])
+        nc.vector.memset(g_sc[:].rearrange("p g n -> p (g n)").bitcast(I32), 0)
+
+        nc.scalar.dma_start(out=r_sc[:], in_=R_scale.rearrange("i j -> (i j)").partition_broadcast(P))
+        for q in range(4):
+            nc.scalar.dma_start(
+                out=g_sc[32 * q : 32 * q + 4, :, :].bitcast(I32),
+                in_=G_scales[:, 4 * q : 4 * q + 4, :].rearrange("g q n -> q g n").bitcast(I32),
+            )
+        nc.sync.dma_start(out=c_sc[:], in_=C_scale.rearrange("(p i) j -> p i j", i=NT))
+        nc.sync.dma_start(out=c_raw[:, 0:2, :], in_=c_v[:, 0:2, :])
+        nc.sync.dma_start(out=g_words[:, :, 0:1024].bitcast(I32), in_=G_words.rearrange("g p n -> p g n")[:, :, 0:1024].bitcast(I32))
+        nc.sync.dma_start(out=s_sb[:, 0, :], in_=s_v[:, 0, :])
+        nc.sync.dma_start(out=g_words[:, :, 1024:2048].bitcast(I32), in_=G_words.rearrange("g p n -> p g n")[:, :, 1024:2048].bitcast(I32))
+        nc.sync.dma_start(out=r_raw[:, 0:1, :], in_=r_v[:, 0:1, :])
+        nc.sync.dma_start(out=g_words[:, :, 2048:3072].bitcast(I32), in_=G_words.rearrange("g p n -> p g n")[:, :, 2048:3072].bitcast(I32))
+        nc.sync.dma_start(out=g_words[:, :, 3072:4096].bitcast(I32), in_=G_words.rearrange("g p n -> p g n")[:, :, 3072:4096].bitcast(I32))
+        nc.sync.dma_start(out=s_sb[:, 1, :], in_=s_v[:, 1, :])
+        nc.sync.dma_start(out=r_raw[:, 1:2, :], in_=r_v[:, 1:2, :])
+        nc.sync.dma_start(out=c_raw[:, 2:5, :], in_=c_v[:, 2:5, :])
+        nc.sync.dma_start(out=s_sb[:, 2, :], in_=s_v[:, 2, :])
+        nc.sync.dma_start(out=r_raw[:, 2:4, :], in_=r_v[:, 2:4, :])
+        nc.sync.dma_start(out=s_sb[:, 3, :], in_=s_v[:, 3, :])
+        nc.sync.dma_start(out=c_raw[:, 5:8, :], in_=c_v[:, 5:8, :])
+        nc.sync.dma_start(out=r_raw[:, 4:6, :], in_=r_v[:, 4:6, :])
+        nc.sync.dma_start(out=s_sb[:, 4, :], in_=s_v[:, 4, :])
+        nc.sync.dma_start(out=r_raw[:, 6:8, :], in_=r_v[:, 6:8, :])
+        nc.sync.dma_start(out=s_sb[:, 5, :], in_=s_v[:, 5, :])
+        nc.sync.dma_start(out=leak_sb[:], in_=leak.partition_broadcast(P))
+        nc.sync.dma_start(out=prev_sb[:, 0:4, :], in_=p_v[:, 0:4, :])
+        nc.sync.dma_start(out=s_sb[:, 6, :], in_=s_v[:, 6, :])
+        nc.sync.dma_start(out=s_sb[:, 7, :], in_=s_v[:, 7, :])
+        nc.sync.dma_start(out=gain_sb[:], in_=gain.partition_broadcast(P))
+        nc.sync.dma_start(out=prev_sb[:, 4:8, :], in_=p_v[:, 4:8, :])
+        def widen(dst, raw, scale, on_vector):
+            if on_vector:
+                nc.vector.tensor_scalar(out=dst, in0=raw.bitcast(FP8), scalar1=scale, scalar2=None, op0=MULT)
+            else:
+                nc.scalar.activation(out=dst, in_=raw.bitcast(FP8), func=COPY, scale=scale)
+
+        def turn(values, groups, dst):
+            words = values.bitcast(F32)
+            for g0 in range(0, groups, 2):
+                bank = psum.tile([P, 2, 2, P], F32, tag="turn", bufs=3, name="bank")
+                for g in range(2):
+                    for u in range(2):
+                        w0 = 256 * (g0 + g) + u
+                        nc.tensor.transpose(bank[:, g, u, :], words[:, w0 : w0 + 255 : 2], ident[:])
+                nc.scalar.copy(
+                    out=dst[:, g0 : g0 + 2, :, :].bitcast(F32),
+                    in_=bank[:].rearrange("p g u r -> p g r u"),
+                )
+
+        c_four = {}
+        c_wide = {}
+
+        def widen_c(i, on_vector):
+            c_wide[i] = work.tile([P, A], BF16, tag="c_wide", bufs=2, align_bytes=64, name="c_w")
+            for j in range(A // P):
+                k = slice(P * j, P * (j + 1))
+                widen(c_wide[i][:, k], c_raw[:, i, k], c_sc[:, i, j : j + 1], on_vector)
+
+        def turn_c(i):
+            c_four[i] = work.tile([P, GA, P, 4], BF16, tag="c_four", bufs=2, align_bytes=64, name="c_f")
+            turn(c_wide[i][:], GA, c_four[i])
+
+        def quant_c(i):
+            nc.vector.quantize_mx(
+                out=c_codes[:, i, :].bitcast(FP8X4),
+                scales=c_planes[:, i, :],
+                in_=c_four[i][:].rearrange("p g r j -> p (g r j)"),
+            )
+
+        r_four = {}
+        r_wide = {}
+
+        def widen_r(i, on_vector):
+            r_wide[i] = work.tile([P, L], BF16, tag="r_wide", bufs=3, align_bytes=64, name="r_w")
+            for j in range(L // P):
+                k = slice(P * j, P * (j + 1))
+                s = i * (L // P) + j
+                widen(r_wide[i][:, k], r_raw[:, i, k], r_sc[:, s : s + 1], on_vector)
+
+        def turn_r(i):
+            r_four[i] = work.tile([P, GL, P, 4], BF16, tag="r_four", bufs=3, align_bytes=64, name="r_f")
+            turn(r_wide[i][:], GL, r_four[i])
+
+        def quant_r(i):
+            cols = slice(P * i, P * (i + 1))
+            for g in range(GL):
+                nc.vector.quantize_mx(
+                    out=r_codes[:, g, cols].bitcast(FP8X4),
+                    scales=r_planes[:, g, cols],
+                    in_=r_four[i][:, g, :, :].rearrange("p r j -> p (r j)"),
+                )
+
+        full = {}
+        f_four = {}
+
+        def mirror(i):
+            full[i] = work.tile([P, GL, 2, P, 2], BF16, tag="full", bufs=2, align_bytes=64, name="full_t")
+            for n in range(NL):
+                acc = psum.tile([P, 512], F32, tag="acc", bufs=3, name="acc")
+                for g in range(GA):
+                    nc.tensor.matmul_mx(
+                        out=acc[:],
+                        lhsT=c_codes[:, i, P * g : P * (g + 1)].bitcast(FP8X4),
+                        lhsT_scale=c_planes[:, i, P * g : P * (g + 1)],
+                        rhs=g_words[:, g, 1024 * n : 1024 * (n + 1)].bitcast(FP4X4),
+                        rhs_scale=g_sc[:, g, 512 * n : 512 * (n + 1)],
+                        start=(g == 0),
+                        stop=(g == GA - 1),
+                    )
+                nc.vector.tensor_tensor(
+                    out=full[i][:, n, :, :, :],
+                    in0=acc[:].rearrange("p (w u e) -> p u w e", u=2, e=2),
+                    in1=s_sb[:, i, 512 * n : 512 * (n + 1)].rearrange("p (w u e) -> p u w e", u=2, e=2),
+                    op=ADD,
+                )
+
+        def turn_f(i):
+            f_four[i] = work.tile([P, GL, P, 4], BF16, tag="f_four", bufs=2, align_bytes=64, name="f_f")
+            words = full[i][:].rearrange("p g u w e -> p (g u w e)").bitcast(F32)
+            for g0 in range(0, GL, 2):
+                bank = psum.tile([P, 2, 2, P], F32, tag="turn", bufs=3, name="bank")
+                for g in range(2):
+                    for u in range(2):
+                        w0 = P * (2 * (g0 + g) + u)
+                        nc.tensor.transpose(bank[:, g, u, :], words[:, w0 : w0 + P], ident[:])
+                nc.scalar.copy(
+                    out=f_four[i][:, g0 : g0 + 2, :, :].bitcast(F32),
+                    in_=bank[:].rearrange("p g u r -> p g r u"),
+                )
+
+        def quant_f(i):
+            nc.vector.quantize_mx(
+                out=f_codes[:, i, :].bitcast(FP8X4),
+                scales=f_planes[:, i, :],
+                in_=f_four[i][:].rearrange("p g r j -> p (g r j)"),
+            )
+
+        left = {}
+
+        def leaky(i):
+            left[i] = work.tile([P, A], F32, tag="left", bufs=8, align_bytes=64, name="left_t")
+            nc.gpsimd.tensor_tensor(out=left[i][:], in0=prev_sb[:, i, :], in1=leak_sb[:], op=MULT)
+
+        def react(i, c):
+            cols = slice(512 * c, 512 * (c + 1))
+            acc2 = psum.tile([P, 512], F32, tag="acc2", bufs=2, name="acc2")
+            for g in range(GL):
+                nc.tensor.matmul_mx(
+                    out=acc2[:],
+                    lhsT=f_codes[:, i, P * g : P * (g + 1)].bitcast(FP8X4),
+                    lhsT_scale=f_planes[:, i, P * g : P * (g + 1)],
+                    rhs=r_codes[:, g, cols].bitcast(FP8X4),
+                    rhs_scale=r_planes[:, g, cols],
+                    start=(g == 0),
+                    stop=(g == GL - 1),
+                )
+            gained[i, c] = work.tile([P, 512], F32, tag="gained", bufs=4, align_bytes=64, name="gained_t")
+            nc.vector.tensor_tensor(out=gained[i, c][:], in0=acc2[:], in1=gain_sb[:, cols], op=MULT)
+
+        gained = {}
+
+        def finish(i, c):
+            cols = slice(512 * c, 512 * (c + 1))
+            nc.vector.tensor_tensor(out=left[i][:, cols], in0=gained[i, c][:], in1=left[i][:, cols], op=ADD)
+            nc.sync.dma_start(out=o_v[:, i, cols], in_=left[i][:, cols])
+
+
+        V_R = (0, 1, 2, 3, 4)
+        TURN_R = [[0], [1, 2], [3], [4], [5], [6], [7], []]
+        REACT = [[], [], [], [], [(0, 0),(1, 0),(2, 0)], [(3, 0),(4, 0)], [(5, 0)], [(6, 0)], [(0, 1),(1, 1),(2, 1),(3, 1),(4, 1),(5, 1),(6, 1), (7, 0), (7, 1)]]
+        LEAKY = [[0], [1], [2], [3], [4], [5], [6], [7]]
+        with tc.manual_schedule():
+            widen_c(0, True)
+            widen_c(1, False)
+            turn_c(0)
+            quant_c(0)
+            turn_c(1)
+            quant_c(1)
+            widen_c(2, False)
+            pend_q = []
+            pend_f = []
+            for i in TURN_R[0]:
+                widen_r(i, i in V_R)
+            for s in range(NT):
+                mirror(s)
+                for i, c in REACT[s]:
+                    react(i, c)
+                if s + 2 < NT:
+                    turn_c(s + 2)
+                for i in TURN_R[s]:
+                    turn_r(i)
+                turn_f(s)
+                if s + 3 < NT:
+                    widen_c(s + 3, False)
+                if s + 1 < NT:
+                    for i in TURN_R[s + 1]:
+                        widen_r(i, i in V_R)
+                for i, c in REACT[s]:
+                    finish(i, c)
+                if s + 2 < NT:
+                    quant_c(s + 2)
+                for i in LEAKY[s]:
+                    leaky(i)
+                for i in TURN_R[s]:
+                    quant_r(i)
+                quant_f(s)
+            last = None
+            for i, c in REACT[NT]:
+                react(i, c)
+                if last:
+                    finish(*last)
+                last = (i, c)
+            finish(*last)

@@ -74,26 +74,28 @@ def tile_leaky_slope_reconstructor_d6_kernel(
         nc.sync.dma_start(out=g_words[:, :, 0:1024].bitcast(I32), in_=G_words.rearrange("g p n -> p g n")[:, :, 0:1024].bitcast(I32))
         nc.sync.dma_start(out=s_sb[:, 0, :], in_=s_v[:, 0, :])
         nc.sync.dma_start(out=g_words[:, :, 1024:2048].bitcast(I32), in_=G_words.rearrange("g p n -> p g n")[:, :, 1024:2048].bitcast(I32))
-        nc.sync.dma_start(out=r_raw[:, 0:1, :], in_=r_v[:, 0:1, :])
         nc.sync.dma_start(out=g_words[:, :, 2048:3072].bitcast(I32), in_=G_words.rearrange("g p n -> p g n")[:, :, 2048:3072].bitcast(I32))
         nc.sync.dma_start(out=g_words[:, :, 3072:4096].bitcast(I32), in_=G_words.rearrange("g p n -> p g n")[:, :, 3072:4096].bitcast(I32))
+        nc.sync.dma_start(out=r_raw[:, 0:1, :], in_=r_v[:, 0:1, :])
         nc.sync.dma_start(out=s_sb[:, 1, :], in_=s_v[:, 1, :])
         nc.sync.dma_start(out=r_raw[:, 1:2, :], in_=r_v[:, 1:2, :])
         nc.sync.dma_start(out=c_raw[:, 2:5, :], in_=c_v[:, 2:5, :])
+        nc.sync.dma_start(out=r_raw[:, 2:3, :], in_=r_v[:, 2:3, :])
         nc.sync.dma_start(out=s_sb[:, 2, :], in_=s_v[:, 2, :])
-        nc.sync.dma_start(out=r_raw[:, 2:4, :], in_=r_v[:, 2:4, :])
+        nc.sync.dma_start(out=leak_sb[:], in_=leak.partition_broadcast(P))
+        nc.sync.dma_start(out=prev_sb[:, 0:2, :], in_=p_v[:, 0:2, :])
+        nc.sync.dma_start(out=r_raw[:, 3:4, :], in_=r_v[:, 3:4, :])
         nc.sync.dma_start(out=s_sb[:, 3, :], in_=s_v[:, 3, :])
-        nc.sync.dma_start(out=c_raw[:, 5:8, :], in_=c_v[:, 5:8, :])
         nc.sync.dma_start(out=r_raw[:, 4:6, :], in_=r_v[:, 4:6, :])
+        nc.sync.dma_start(out=prev_sb[:, 2:4, :], in_=p_v[:, 2:4, :])
+        nc.sync.dma_start(out=c_raw[:, 5:8, :], in_=c_v[:, 5:8, :])
         nc.sync.dma_start(out=s_sb[:, 4, :], in_=s_v[:, 4, :])
         nc.sync.dma_start(out=r_raw[:, 6:8, :], in_=r_v[:, 6:8, :])
         nc.sync.dma_start(out=s_sb[:, 5, :], in_=s_v[:, 5, :])
-        nc.sync.dma_start(out=leak_sb[:], in_=leak.partition_broadcast(P))
-        nc.sync.dma_start(out=prev_sb[:, 0:4, :], in_=p_v[:, 0:4, :])
-        nc.sync.dma_start(out=s_sb[:, 6, :], in_=s_v[:, 6, :])
-        nc.sync.dma_start(out=s_sb[:, 7, :], in_=s_v[:, 7, :])
         nc.sync.dma_start(out=gain_sb[:], in_=gain.partition_broadcast(P))
         nc.sync.dma_start(out=prev_sb[:, 4:8, :], in_=p_v[:, 4:8, :])
+        nc.sync.dma_start(out=s_sb[:, 6, :], in_=s_v[:, 6, :])
+        nc.sync.dma_start(out=s_sb[:, 7, :], in_=s_v[:, 7, :])
         def widen(dst, raw, scale, on_vector):
             if on_vector:
                 nc.vector.tensor_scalar(out=dst, in0=raw.bitcast(FP8), scalar1=scale, scalar2=None, op0=MULT)
@@ -205,7 +207,7 @@ def tile_leaky_slope_reconstructor_d6_kernel(
 
         def leaky(i):
             left[i] = work.tile([P, A], F32, tag="left", bufs=8, align_bytes=64, name="left_t")
-            nc.gpsimd.tensor_tensor(out=left[i][:], in0=prev_sb[:, i, :], in1=leak_sb[:], op=MULT)
+            nc.vector.tensor_tensor(out=left[i][:], in0=prev_sb[:, i, :], in1=leak_sb[:], op=MULT)
 
         def react(i, c):
             cols = slice(512 * c, 512 * (c + 1))
@@ -231,11 +233,11 @@ def tile_leaky_slope_reconstructor_d6_kernel(
             nc.sync.dma_start(out=o_v[:, i, cols], in_=left[i][:, cols])
 
 
-        V_R = (0, 1, 2, 3, 4)
+        V_R = (0, 1)
         TURN_R = [[0], [1, 2], [3], [4], [5], [6], [7], []]
         REACT = [[], [], [], [], [(0, 0),(1, 0),(2, 0)], [(3, 0),(4, 0)], [(5, 0)], [(6, 0)], [(0, 1),(1, 1),(2, 1),(3, 1),(4, 1),(5, 1),(6, 1), (7, 0), (7, 1)]]
-        LEAKY = [[0], [1], [2], [3], [4], [5], [6], [7]]
-        with tc.manual_schedule():
+        LEAKY = [[], [0], [1], [2], [3, 4], [5], [6], [7]]
+        if True:
             widen_c(0, True)
             widen_c(1, False)
             turn_c(0)

from contextlib import ExitStack

import concourse.mybir as mybir
from concourse.masks import make_identity

T, A, L = 1024, 1024, 2048
P = 128
FLOPS = 2 * T * A * L * 2

F32 = mybir.dt.float32
BF16 = mybir.dt.bfloat16
I32 = mybir.dt.int32
U32 = mybir.dt.uint32
U8 = mybir.dt.uint8
FP8 = mybir.dt.float8_e4m3fn
FP8X4 = mybir.dt.float8_e4m3fn_x4
FP4X4 = mybir.dt.float4_e2m1fn_x4
MULT = mybir.AluOpType.mult
ADD = mybir.AluOpType.add
COPY = mybir.ActivationFunctionType.Copy

NT = T // P
NR = A // P
GA = A // 512
GL = L // 512
NL = L // 512
NA = A // 512


def tile_leaky_slope_reconstructor_d6_kernel(
    tc, C_bytes, C_scale, G_words, G_scales, slopes, R_bytes, R_scale, gain, leak, prev, out
):
    nc = tc.nc
    with ExitStack() as ctx:
        keep = ctx.enter_context(tc.tile_pool(name="keep", bufs=1))
        work = ctx.enter_context(tc.tile_pool(name="work", bufs=3))
        psum = ctx.enter_context(tc.psum_pool(name="psum", bufs=1))

        c_raw = keep.tile([P, NT, A], U8, align_bytes=64)
        c_sc = keep.tile([P, NT, A // P], F32, align_bytes=64)
        g_words = keep.tile([P, GA, 2 * L], U8, align_bytes=64)
        g_sc = keep.tile([P, GA, L], U8, align_bytes=64)
        r_raw = keep.tile([P, NR, L], U8, align_bytes=64)
        r_sc = keep.tile([P, NR * (L // P)], F32, align_bytes=64)
        s_sb = keep.tile([P, NT, L], BF16, align_bytes=64)
        prev_sb = keep.tile([P, NT, A], BF16, align_bytes=64)
        gain_sb = keep.tile([P, A], BF16, align_bytes=64)
        leak_sb = keep.tile([P, A], BF16, align_bytes=64)
        ident = keep.tile([P, P], F32, align_bytes=64)
        c_codes = keep.tile([P, NT, GA * P], U32, align_bytes=64)
        c_planes = keep.tile([P, NT, GA * P], U8, align_bytes=64)
        r_codes = keep.tile([P, GL, A], U32, align_bytes=64)
        r_planes = keep.tile([P, GL, A], U8, align_bytes=64)
        f_codes = keep.tile([P, NT, GL * P], U32, align_bytes=64)
        f_planes = keep.tile([P, NT, GL * P], U8, align_bytes=64)

        c_v = C_bytes.rearrange("(p i) k -> p i k", i=NT)
        s_v = slopes.rearrange("(p i) l -> p i l", i=NT)
        p_v = prev.rearrange("(p i) a -> p i a", i=NT)
        o_v = out.rearrange("(p i) a -> p i a", i=NT)
        r_v = R_bytes.rearrange("(i p) l -> p i l", p=P)

        make_identity(nc, ident[:])
        nc.vector.memset(g_sc[:].rearrange("p g n -> p (g n)").bitcast(I32), 0)

        nc.scalar.dma_start(out=r_sc[:], in_=R_scale.rearrange("i j -> (i j)").partition_broadcast(P))
        for q in range(4):
            nc.scalar.dma_start(
                out=g_sc[32 * q : 32 * q + 4, :, :].bitcast(I32),
                in_=G_scales[:, 4 * q : 4 * q + 4, :].rearrange("g q n -> q g n").bitcast(I32),
            )
        nc.sync.dma_start(out=c_sc[:], in_=C_scale.rearrange("(p i) j -> p i j", i=NT))
        nc.sync.dma_start(out=c_raw[:, 0:2, :], in_=c_v[:, 0:2, :])
        nc.sync.dma_start(out=g_words[:, :, 0:1024].bitcast(I32), in_=G_words.rearrange("g p n -> p g n")[:, :, 0:1024].bitcast(I32))
        nc.sync.dma_start(out=s_sb[:, 0, :], in_=s_v[:, 0, :])
        nc.sync.dma_start(out=g_words[:, :, 1024:2048].bitcast(I32), in_=G_words.rearrange("g p n -> p g n")[:, :, 1024:2048].bitcast(I32))
        nc.sync.dma_start(out=g_words[:, :, 2048:3072].bitcast(I32), in_=G_words.rearrange("g p n -> p g n")[:, :, 2048:3072].bitcast(I32))
        nc.sync.dma_start(out=g_words[:, :, 3072:4096].bitcast(I32), in_=G_words.rearrange("g p n -> p g n")[:, :, 3072:4096].bitcast(I32))
        nc.sync.dma_start(out=r_raw[:, 0:1, :], in_=r_v[:, 0:1, :])
        nc.sync.dma_start(out=s_sb[:, 1, :], in_=s_v[:, 1, :])
        nc.sync.dma_start(out=r_raw[:, 1:2, :], in_=r_v[:, 1:2, :])
        nc.sync.dma_start(out=c_raw[:, 2:5, :], in_=c_v[:, 2:5, :])
        nc.sync.dma_start(out=r_raw[:, 2:3, :], in_=r_v[:, 2:3, :])
        nc.sync.dma_start(out=s_sb[:, 2, :], in_=s_v[:, 2, :])
        nc.sync.dma_start(out=leak_sb[:], in_=leak.partition_broadcast(P))
        nc.sync.dma_start(out=prev_sb[:, 0:2, :], in_=p_v[:, 0:2, :])
        nc.sync.dma_start(out=r_raw[:, 3:4, :], in_=r_v[:, 3:4, :])
        nc.sync.dma_start(out=s_sb[:, 3, :], in_=s_v[:, 3, :])
        nc.sync.dma_start(out=r_raw[:, 4:6, :], in_=r_v[:, 4:6, :])
        nc.sync.dma_start(out=prev_sb[:, 2:4, :], in_=p_v[:, 2:4, :])
        nc.sync.dma_start(out=c_raw[:, 5:8, :], in_=c_v[:, 5:8, :])
        nc.sync.dma_start(out=s_sb[:, 4, :], in_=s_v[:, 4, :])
        nc.sync.dma_start(out=r_raw[:, 6:8, :], in_=r_v[:, 6:8, :])
        nc.sync.dma_start(out=s_sb[:, 5, :], in_=s_v[:, 5, :])
        nc.sync.dma_start(out=gain_sb[:], in_=gain.partition_broadcast(P))
        nc.sync.dma_start(out=prev_sb[:, 4:8, :], in_=p_v[:, 4:8, :])
        nc.sync.dma_start(out=s_sb[:, 6, :], in_=s_v[:, 6, :])
        nc.sync.dma_start(out=s_sb[:, 7, :], in_=s_v[:, 7, :])
        def widen(dst, raw, scale, on_vector):
            if on_vector:
                nc.vector.tensor_scalar(out=dst, in0=raw.bitcast(FP8), scalar1=scale, scalar2=None, op0=MULT)
            else:
                nc.scalar.activation(out=dst, in_=raw.bitcast(FP8), func=COPY, scale=scale)

        def turn(values, groups, dst):
            words = values.bitcast(F32)
            for g0 in range(0, groups, 2):
                bank = psum.tile([P, 2, 2, P], F32, tag="turn", bufs=3, name="bank")
                for g in range(2):
                    for u in range(2):
                        w0 = 256 * (g0 + g) + u
                        nc.tensor.transpose(bank[:, g, u, :], words[:, w0 : w0 + 255 : 2], ident[:])
                nc.scalar.copy(
                    out=dst[:, g0 : g0 + 2, :, :].bitcast(F32),
                    in_=bank[:].rearrange("p g u r -> p g r u"),
                )

        c_four = {}
        c_wide = {}

        def widen_c(i, on_vector):
            c_wide[i] = work.tile([P, A], BF16, tag="c_wide", bufs=2, align_bytes=64, name="c_w")
            for j in range(A // P):
                k = slice(P * j, P * (j + 1))
                widen(c_wide[i][:, k], c_raw[:, i, k], c_sc[:, i, j : j + 1], on_vector)

        def turn_c(i):
            c_four[i] = work.tile([P, GA, P, 4], BF16, tag="c_four", bufs=2, align_bytes=64, name="c_f")
            turn(c_wide[i][:], GA, c_four[i])

        def quant_c(i):
            nc.vector.quantize_mx(
                out=c_codes[:, i, :].bitcast(FP8X4),
                scales=c_planes[:, i, :],
                in_=c_four[i][:].rearrange("p g r j -> p (g r j)"),
            )

        r_four = {}
        r_wide = {}

        def widen_r(i, on_vector):
            r_wide[i] = work.tile([P, L], BF16, tag="r_wide", bufs=3, align_bytes=64, name="r_w")
            for j in range(L // P):
                k = slice(P * j, P * (j + 1))
                s = i * (L // P) + j
                widen(r_wide[i][:, k], r_raw[:, i, k], r_sc[:, s : s + 1], on_vector)

        def turn_r(i):
            r_four[i] = work.tile([P, GL, P, 4], BF16, tag="r_four", bufs=3, align_bytes=64, name="r_f")
            turn(r_wide[i][:], GL, r_four[i])

        def quant_r(i):
            cols = slice(P * i, P * (i + 1))
            for g in range(GL):
                nc.vector.quantize_mx(
                    out=r_codes[:, g, cols].bitcast(FP8X4),
                    scales=r_planes[:, g, cols],
                    in_=r_four[i][:, g, :, :].rearrange("p r j -> p (r j)"),
                )

        full = {}
        f_four = {}

        def mirror(i):
            full[i] = work.tile([P, GL, 2, P, 2], BF16, tag="full", bufs=2, align_bytes=64, name="full_t")
            for n in range(NL):
                acc = psum.tile([P, 512], F32, tag="acc", bufs=3, name="acc")
                for g in range(GA):
                    nc.tensor.matmul_mx(
                        out=acc[:],
                        lhsT=c_codes[:, i, P * g : P * (g + 1)].bitcast(FP8X4),
                        lhsT_scale=c_planes[:, i, P * g : P * (g + 1)],
                        rhs=g_words[:, g, 1024 * n : 1024 * (n + 1)].bitcast(FP4X4),
                        rhs_scale=g_sc[:, g, 512 * n : 512 * (n + 1)],
                        start=(g == 0),
                        stop=(g == GA - 1),
                    )
                nc.vector.tensor_tensor(
                    out=full[i][:, n, :, :, :],
                    in0=acc[:].rearrange("p (w u e) -> p u w e", u=2, e=2),
                    in1=s_sb[:, i, 512 * n : 512 * (n + 1)].rearrange("p (w u e) -> p u w e", u=2, e=2),
                    op=ADD,
                )

        def turn_f(i):
            f_four[i] = work.tile([P, GL, P, 4], BF16, tag="f_four", bufs=2, align_bytes=64, name="f_f")
            words = full[i][:].rearrange("p g u w e -> p (g u w e)").bitcast(F32)
            for g0 in range(0, GL, 2):
                bank = psum.tile([P, 2, 2, P], F32, tag="turn", bufs=3, name="bank")
                for g in range(2):
                    for u in range(2):
                        w0 = P * (2 * (g0 + g) + u)
                        nc.tensor.transpose(bank[:, g, u, :], words[:, w0 : w0 + P], ident[:])
                nc.scalar.copy(
                    out=f_four[i][:, g0 : g0 + 2, :, :].bitcast(F32),
                    in_=bank[:].rearrange("p g u r -> p g r u"),
                )

        def quant_f(i):
            nc.vector.quantize_mx(
                out=f_codes[:, i, :].bitcast(FP8X4),
                scales=f_planes[:, i, :],
                in_=f_four[i][:].rearrange("p g r j -> p (g r j)"),
            )

        left = {}

        def leaky(i):
            left[i] = work.tile([P, A], F32, tag="left", bufs=8, align_bytes=64, name="left_t")
            nc.vector.tensor_tensor(out=left[i][:], in0=prev_sb[:, i, :], in1=leak_sb[:], op=MULT)

        def react(i, c):
            cols = slice(512 * c, 512 * (c + 1))
            acc2 = psum.tile([P, 512], F32, tag="acc2", bufs=2, name="acc2")
            for g in range(GL):
                nc.tensor.matmul_mx(
                    out=acc2[:],
                    lhsT=f_codes[:, i, P * g : P * (g + 1)].bitcast(FP8X4),
                    lhsT_scale=f_planes[:, i, P * g : P * (g + 1)],
                    rhs=r_codes[:, g, cols].bitcast(FP8X4),
                    rhs_scale=r_planes[:, g, cols],
                    start=(g == 0),
                    stop=(g == GL - 1),
                )
            gained[i, c] = work.tile([P, 512], F32, tag="gained", bufs=4, align_bytes=64, name="gained_t")
            nc.vector.tensor_tensor(out=gained[i, c][:], in0=acc2[:], in1=gain_sb[:, cols], op=MULT)

        gained = {}

        def finish(i, c):
            cols = slice(512 * c, 512 * (c + 1))
            nc.vector.tensor_tensor(out=left[i][:, cols], in0=gained[i, c][:], in1=left[i][:, cols], op=ADD)
            nc.sync.dma_start(out=o_v[:, i, cols], in_=left[i][:, cols])


        V_R = (0, 1)
        TURN_R = [[0], [1, 2], [3], [4], [5], [6], [7], []]
        REACT = [[], [], [], [], [(0, 0),(1, 0),(2, 0)], [(3, 0),(4, 0)], [(5, 0)], [(6, 0)], [(0, 1),(1, 1),(2, 1),(3, 1),(4, 1),(5, 1),(6, 1), (7, 0), (7, 1)]]
        LEAKY = [[], [0], [1], [2], [3, 4], [5], [6], [7]]
        if True:
            widen_c(0, True)
            widen_c(1, False)
            turn_c(0)
            quant_c(0)
            turn_c(1)
            quant_c(1)
            widen_c(2, False)
            pend_q = []
            pend_f = []
            for i in TURN_R[0]:
                widen_r(i, i in V_R)
            for s in range(NT):
                mirror(s)
                for i, c in REACT[s]:
                    react(i, c)
                if s + 2 < NT:
                    turn_c(s + 2)
                for i in TURN_R[s]:
                    turn_r(i)
                turn_f(s)
                if s + 3 < NT:
                    widen_c(s + 3, False)
                if s + 1 < NT:
                    for i in TURN_R[s + 1]:
                        widen_r(i, i in V_R)
                for i, c in REACT[s]:
                    finish(i, c)
                if s + 2 < NT:
                    quant_c(s + 2)
                for i in LEAKY[s]:
                    leaky(i)
                for i in TURN_R[s]:
                    quant_r(i)
                quant_f(s)
            last = None
            for i, c in REACT[NT]:
                react(i, c)
                if last:
                    finish(*last)
                last = (i, c)
            finish(*last)
